import numpy as np
import ml_dtypes


def mxq(x, axis, fmt="e4m3"):
    dtype, down = {"e4m3": (ml_dtypes.float8_e4m3fn, 7), "e5m2": (ml_dtypes.float8_e5m2, 14)}[fmt]
    v = np.moveaxis(np.asarray(x, np.float32).astype(ml_dtypes.bfloat16).astype(np.float64), axis, -1)
    blocks = v.reshape(v.shape[:-1] + (-1, 32))
    amax = np.abs(blocks).max(-1, keepdims=True)
    byte = np.maximum(np.where(amax > 0, np.frexp(amax)[1] - 1 + 127, 0) - down, 1)
    scale = np.exp2(byte - 127.0)
    codes = (blocks / scale).astype(np.float32).astype(dtype).astype(np.float64)
    return np.moveaxis((codes * scale).reshape(v.shape), -1, axis)


WIDE = False


def mx_kscale(k):
    if not WIDE:
        return np.ones(k)
    levels = np.array([10, -10, 5, -5, 0])
    if k % 512:
        return np.exp2(np.random.permutation(np.resize(levels, k // 32))).repeat(32)
    a = np.empty((k // 512, 16))
    for p in range(k // 512):
        a[p, :8] = np.random.permutation(np.resize(levels, 8))
        for g in range(8):
            far = levels[np.abs(levels - a[p, g]) >= 10]
            a[p, g + 8] = far[np.random.randint(len(far))]
    return np.exp2(a.ravel()).repeat(32)


def f64(x):
    return np.asarray(x).astype(np.float64)


def striped(idx):
    return np.tile(idx.reshape(-1, 16).T, (8, 1)).astype(np.uint16)


def unstriped(offs):
    return offs[:16].T.reshape(-1).astype(np.int64)


def striped8(idx):
    return np.concatenate([x.reshape(-1, 16).T for x in idx]).astype(np.uint16)


def runs(offs, k):
    lists = np.stack([offs[16 * r : 16 * r + 16].T.reshape(-1) for r in range(8)]).astype(np.int64)
    return lists[np.arange(k) % 512 // 64]


def pack_weight(w):
    k, n = w.shape
    w = f64(np.asarray(w, np.float32).astype(ml_dtypes.bfloat16)).reshape(k // 32, 32, n)
    amax = np.abs(w).max(1)
    byte = np.clip(np.where(amax > 0, np.frexp(amax)[1] - 1 + 127 - 7, 1), 1, 254)
    scaled = (w * np.exp2(127.0 - byte)[:, None, :]).reshape(k, n).astype(np.float32)
    words = np.ascontiguousarray(scaled.reshape(k // 512, 128, 4, n).transpose(0, 1, 3, 2)).astype(ml_dtypes.float8_e4m3fn).view(np.uint8)
    return words, np.ascontiguousarray(byte.astype(np.uint8).reshape(k // 512, 16, n))


def unpack_weight(words, scales):
    g, p, n, _ = words.shape
    vals = np.ascontiguousarray(words).view(ml_dtypes.float8_e4m3fn).astype(np.float64) * np.repeat(np.exp2(scales.astype(np.float64) - 127.0), 8, axis=1)[..., None]
    return vals.transpose(0, 1, 3, 2).reshape(g * 512, n)


E2M1 = np.array([0.0, 0.5, 1.0, 1.5, 2.0, 3.0, 4.0, 6.0, -0.0, -0.5, -1.0, -1.5, -2.0, -3.0, -4.0, -6.0])


def pack_fp4(w):
    k, n = w.shape
    w = f64(np.asarray(w, np.float32).astype(ml_dtypes.bfloat16)).reshape(k // 32, 32, n)
    amax = np.abs(w).max(1)
    mant, ex = np.frexp(amax / 6.0)
    byte = np.clip(np.where(amax > 0, np.where(mant > 0.5, ex, ex - 1) + 127, 1), 1, 254)
    scaled = (w * np.exp2(127.0 - byte)[:, None, :]).reshape(k, n).astype(np.float32)
    c = np.ascontiguousarray(scaled.reshape(k // 512, 128, 4, n).transpose(0, 1, 3, 2)).astype(ml_dtypes.float4_e2m1fn).view(np.uint8) & 0xF
    words = (c[..., 0::2] | (c[..., 1::2] << 4)).reshape(k // 512, 128, 2 * n)
    return np.ascontiguousarray(words), np.ascontiguousarray(byte.astype(np.uint8).reshape(k // 512, 16, n))


def unpack_fp4(words, scales):
    g, _, n = scales.shape
    words = np.ascontiguousarray(words).reshape(g, 128, n, 2)
    nib = np.empty((g, 128, n, 4), np.uint8)
    nib[..., 0::2] = words & 0xF
    nib[..., 1::2] = words >> 4
    vals = E2M1[nib] * np.repeat(np.exp2(scales.astype(np.float64) - 127.0), 8, axis=1)[..., None]
    return vals.transpose(0, 1, 3, 2).reshape(g * 512, n)


def planes(y):
    n, m = y.shape
    v = y.astype(np.float32).astype(ml_dtypes.bfloat16).astype(np.float64).reshape(n // 32, 32, m)
    top = np.abs(v).max(1)
    byte = np.clip(np.where(top > 0, np.frexp(top)[1] - 1 + 127 - 7, 1), 1, 254)
    codes = (v * np.exp2(127.0 - byte)[:, None, :]).reshape(n, m).astype(np.float32).astype(ml_dtypes.float8_e4m3fn).view(np.uint8)
    words = codes.reshape(n // 512, 128, 4, m).transpose(0, 1, 3, 2)
    return np.ascontiguousarray(words), np.ascontiguousarray(byte.astype(np.uint8).reshape(n // 512, 16, m))


K, T, S, N, G, H = 512, 2048, 512, 512, 2048, 512


def setup_inputs():
    n = np.random.standard_normal
    s = mx_kscale(K)[:, None]
    u = mx_kscale(S)
    packed_xT = pack_weight(n((K, T)) * s)
    packed_dT = pack_weight(n((K, G)) / s)
    packed_w1 = pack_fp4(n((H, N)) / np.sqrt(H) / u[:, None])
    return {
        "x_words": packed_xT[0],
        "x_scales": packed_xT[1],
        "d_words": packed_dT[0],
        "d_scales": packed_dT[1],
        "gn": (np.random.uniform(0.5, 1.5, (H, 1)) * u[:, None]).astype(np.float32),
        "w1_words": packed_w1[0],
        "w1_scales": packed_w1[1],
        "offs": striped(np.random.permutation(T)[:S]),
        "kidx": striped8(np.random.randint(0, G, (8, H))),
        "n1": striped8(np.stack([np.random.permutation(S) for _ in range(8)])),
        "n2": striped8(np.stack([np.random.permutation(S) for _ in range(8)])),
        "n3": striped8(np.stack([np.random.permutation(S) for _ in range(8)])),
        "n4": striped8(np.stack([np.random.permutation(S) for _ in range(8)])),
        "n5": striped8(np.stack([np.random.permutation(S) for _ in range(8)])),
    }


def reference(x_words, x_scales, d_words, d_scales, gn, w1_words, w1_scales, offs, kidx, n1, n2, n3, n4, n5):
    d_kidx = unpack_weight(d_words, d_scales)[np.arange(K)[:, None], runs(kidx, K)]
    xq = unpack_weight(x_words, x_scales)[:, unstriped(offs)]
    s = 0.0625 * (d_kidx.T @ xq)
    z = f64(gn) * (s + s[np.arange(H)[:, None], runs(n1, H)] - (np.maximum(s[np.arange(H)[:, None], runs(n2, H)], s[np.arange(H)[:, None], runs(n3, H)])))
    h = unpack_fp4(w1_words, w1_scales).T @ mxq(z, 0, "e4m3")
    out_0 = (h[np.arange(N)[:, None], runs(n4, N)]) / (np.abs(h) + np.abs(h[np.arange(N)[:, None], runs(n5, N)]) + 0.5)
    return (out_0,) + planes(out_0)

@@ -1,0 +1,290 @@
+from contextlib import ExitStack
+
+import concourse.mybir as mybir
+
+K, T, S, N, G, H = 512, 2048, 512, 512, 2048, 512
+FLOPS = 2 * K * H * S + 2 * H * N * S
+
+F32 = mybir.dt.float32
+BF16 = mybir.dt.bfloat16
+I32 = mybir.dt.int32
+U32 = mybir.dt.uint32
+U16 = mybir.dt.uint16
+U8 = mybir.dt.uint8
+FP8X4 = mybir.dt.float8_e4m3fn_x4
+FP4X4 = mybir.dt.float4_e2m1fn_x4
+ALU = mybir.AluOpType
+ACT = mybir.ActivationFunctionType
+
+P = 128
+PACK = 4
+PIECES_Z = ((0, 256), (256, 384), (384, 512))
+PIECES_OUT = ((0, 256), (256, 384), (384, 512))
+
+
+def tile_picked_keytrimnorm2_none_po_kernel(
+    tc, x_words, x_scales, d_words, d_scales, gn, w1_words, w1_scales,
+    offs, kidx, n1, n2, n3, n4, n5, out_0, out_1, out_2,
+):
+    nc = tc.nc
+    with ExitStack() as ctx:
+        keep = ctx.enter_context(tc.tile_pool(name="keep", bufs=1))
+        ring = ctx.enter_context(tc.tile_pool(name="ring", bufs=4))
+        psum = ctx.enter_context(tc.psum_pool(name="psum", bufs=1))
+
+        def held(shape, dtype, name):
+            return keep.tile(shape, dtype, name=name, align_bytes=64)
+
+        def load_list(src, name):
+            tile = keep.tile([P, S // 16], U16, name=name)
+            nc.sync.dma_start(tile[:], src)
+            return tile
+
+        def entries(lst, lo, hi):
+            return lst[:, lo // 16 : hi // 16]
+
+        d_bytes = held([P, G], U8, "d_bytes")
+        x_bytes = held([P, T], U8, "x_bytes")
+        w_bytes = held([P, N], U8, "w_bytes")
+        nc.vector.memset(d_bytes[:].bitcast(I32), 0)
+        nc.vector.memset(x_bytes[:].bitcast(I32), 0)
+        nc.gpsimd.memset(w_bytes[:].bitcast(I32), 0)
+        four = held([P, 1], F32, "four")
+        nc.vector.memset(four[:], 4.0)
+
+        kidx_sb = load_list(kidx, "kidx_sb")
+        nc.sync.dma_start(d_bytes[:].bitcast(I32)[0:P:8, :], d_scales[0].bitcast(I32))
+        offs_sb = load_list(offs, "offs_sb")
+        x_rows = x_scales[0].bitcast(I32)
+        for q in range(4):
+            nc.scalar.dma_start(x_bytes[:].bitcast(I32)[32 * q : 32 * q + 4, :], x_rows[4 * q : 4 * q + 4, :])
+        half = held([P, 1], F32, "half")
+        nc.scalar.activation(half[:], four[:], ACT.Abs_reciprocal_sqrt)
+        d_table = held([P, G], U32, "d_table")
+        nc.sync.dma_start(d_table[:].bitcast(I32), d_words[0].rearrange("p n r -> p (n r)").bitcast(I32))
+        x_table = held([P, T], U32, "x_table")
+        nc.sync.dma_start(x_table[:].bitcast(I32), x_words[0].rearrange("p n r -> p (n r)").bitcast(I32))
+        n1_sb = load_list(n1, "n1_sb")
+        n2_sb = load_list(n2, "n2_sb")
+        n3_sb = load_list(n3, "n3_sb")
+        gain = held([P, PACK], F32, "gain")
+        nc.sync.dma_start(gain[:], gn.rearrange("(p t) o -> p (t o)", t=PACK))
+        w_table = held([P, 2 * N], U8, "w_table")
+        nc.sync.dma_start(w_table[:].bitcast(I32), w1_words[0].bitcast(I32))
+        w_rows = w1_scales[0].bitcast(I32)
+        for q in range(4):
+            nc.sync.dma_start(w_bytes[:].bitcast(I32)[32 * q : 32 * q + 4, :], w_rows[4 * q : 4 * q + 4, :])
+        n5_sb = load_list(n5, "n5_sb")
+        n4_sb = load_list(n4, "n4_sb")
+
+        key_bytes = held([P, H], U8, "key_bytes")
+        nc.vector.tensor_copy(key_bytes[:], d_bytes[:].indirect(kidx_sb[:]))
+        key_bytes_dealt = held([P, H], U8, "key_bytes_dealt")
+        nc.vector.tensor_copy(
+            key_bytes_dealt[:].rearrange("p (t m) -> p t m", t=PACK),
+            key_bytes[:].rearrange("p (m t) -> p t m", t=PACK),
+        )
+        key_scale = held([P, H], U8, "key_scale")
+        nc.vector.tensor_copy(key_scale[:].bitcast(I32), key_bytes_dealt[:].bitcast(I32))
+        for r in range(1, 4):
+            nc.scalar.dma_start(
+                key_scale[:].bitcast(I32)[r:P:32, :], key_bytes_dealt[:].bitcast(I32)[8 * r : P : 32, :]
+            )
+        query_scale = held([P, S], U8, "query_scale")
+        nc.vector.tensor_copy(query_scale[:], x_bytes[:].indirect(offs_sb[:]))
+        key_words = held([P, H], U32, "key_words")
+        nc.vector.tensor_copy(key_words[:], d_table[:].indirect(kidx_sb[:]))
+        key_dealt = held([P, H], U32, "key_dealt")
+        nc.vector.tensor_copy(
+            key_dealt[:].bitcast(I32).rearrange("p (t m) -> p t m", t=PACK),
+            key_words[:].bitcast(I32).rearrange("p (m t) -> p t m", t=PACK),
+        )
+        query_words = held([P, S], U32, "query_words")
+        for lo, hi in ((0, 256), (256, 512)):
+            nc.vector.tensor_copy(query_words[:, lo:hi], x_table[:].indirect(entries(offs_sb, lo, hi)))
+
+        w_dealt = held([P, 2 * N], U8, "w_dealt")
+        nc.vector.tensor_copy(
+            w_dealt[:].rearrange("p (t m b) -> p t m b", t=PACK, b=2),
+            w_table[:].rearrange("p (m t b) -> p t m b", t=PACK, b=2),
+        )
+        w_scale = held([P, N], U8, "w_scale")
+        nc.vector.tensor_copy(
+            w_scale[:].rearrange("p (t m) -> p t m", t=PACK),
+            w_bytes[:].rearrange("p (m t) -> p t m", t=PACK),
+        )
+        factor = held([P, PACK], F32, "factor")
+        nc.scalar.activation(factor[:], gain[:], ACT.Copy, scale=-0.0625)
+
+        def score_matmul(bank, t, lo, hi):
+            acc = psum.tile([P, hi - lo], F32, tag=f"bank{bank}", name=f"score{t}_{lo}")
+            nc.tensor.matmul_mx(
+                out=acc[:],
+                lhsT=key_dealt[:, t * P : (t + 1) * P].bitcast(FP8X4),
+                lhsT_scale=key_scale[:, t * P : (t + 1) * P],
+                rhs=query_words[:, lo:hi].bitcast(FP8X4),
+                rhs_scale=query_scale[:, lo:hi],
+                start=True,
+                stop=True,
+            )
+            return acc
+
+        score = [held([P, S], F32, f"score_window{t}") for t in range(PACK)]
+        score_plain = [held([P, S], F32, f"score_plain{t}") for t in range(PACK)]
+        first = score_matmul(0, 0, 0, 256)
+        second = score_matmul(1, 0, 256, 512)
+        rest = [score_matmul(1 + t, t, 0, S) for t in range(1, PACK)]
+        nc.scalar.copy(score[0][:, 0:256], first[:])
+        nc.scalar.copy(score_plain[0][:, 0:256], first[:])
+        nc.scalar.copy(score[0][:, 256:512], second[:])
+        for t in range(1, PACK):
+            nc.scalar.copy(score[t][:], rest[t - 1][:])
+            nc.scalar.copy(score_plain[t][:, 0:256], rest[t - 1][:, 0:256])
+        nc.scalar.copy(score_plain[0][:, 256:512], second[:])
+        for t in range(1, PACK):
+            nc.scalar.copy(score_plain[t][:, 256:512], rest[t - 1][:, 256:512])
+
+        h_window = [held([P, S], F32, f"h_window{t}") for t in range(PACK)]
+        size_window = [held([P, S], F32, f"size_window{t}") for t in range(PACK)]
+        size_plain = held([P, PACK, S], F32, "size_plain")
+        z_words = held([P, S], U32, "z_words")
+        z_scale = held([P, S], U8, "z_scale")
+        z_grouped = [held([P, hi - lo, PACK], BF16, f"z_grouped{lo}") for lo, hi in PIECES_Z]
+        h_banks = ((5, 5, 6, 6), (7, 7, 7, 7), (0, 1, 2, 3))
+
+        units = [(c, t) for c in range(len(PIECES_Z)) for t in range(PACK)]
+        sums = {}
+        gaps = {}
+
+        def gather_sum(u):
+            c, t = units[u]
+            lo, hi = PIECES_Z[c]
+            sums[u] = ring.tile([P, hi - lo], F32, tag="sum", name=f"sum{u}")
+            nc.vector.tensor_tensor(
+                sums[u][:], score[t][:].indirect(entries(n1_sb, lo, hi)), score_plain[t][:, lo:hi], ALU.add
+            )
+
+        def gather_gaps(u):
+            c, t = units[u]
+            lo, hi = PIECES_Z[c]
+            gaps[u] = []
+            for name, lst in (("gap2", n2_sb), ("gap3", n3_sb)):
+                gap = ring.tile([P, hi - lo], F32, tag=name, name=f"{name}_{u}")
+                nc.vector.tensor_tensor(gap[:], score[t][:].indirect(entries(lst, lo, hi)), sums[u][:], ALU.subtract)
+                gaps[u].append(gap)
+
+        def larger_gap(u):
+            c, t = units[u]
+            lo, hi = PIECES_Z[c]
+            larger = ring.tile([P, hi - lo], F32, tag="larger", name=f"larger{u}")
+            nc.vector.tensor_tensor(larger[:], gaps[u][0][:], gaps[u][1][:], ALU.max)
+            nc.scalar.activation(z_grouped[c][:, :, t], larger[:], ACT.Copy, scale=factor[:, t : t + 1])
+
+        def second_product(c):
+            lo, hi = PIECES_Z[c]
+            w = hi - lo
+            nc.vector.quantize_mx(
+                out=z_words[:, lo:hi].bitcast(FP8X4),
+                scales=z_scale[:, lo:hi],
+                in_=z_grouped[c][:].rearrange("p n t -> p (n t)"),
+            )
+            banks = {}
+            parts = []
+            for t in range(PACK):
+                b = h_banks[c][t]
+                members = [m for m in range(PACK) if h_banks[c][m] == b]
+                if b not in banks:
+                    banks[b] = psum.tile([P, len(members), w], F32, tag=f"bank{b}", name=f"h{c}_{b}")
+                part = banks[b][:, t - members[0], :]
+                parts.append(part)
+                nc.tensor.matmul_mx(
+                    out=part,
+                    lhsT=w_dealt[:, 2 * t * P : 2 * (t + 1) * P].bitcast(FP4X4),
+                    lhsT_scale=w_scale[:, t * P : (t + 1) * P],
+                    rhs=z_words[:, lo:hi].bitcast(FP8X4),
+                    rhs_scale=z_scale[:, lo:hi],
+                    start=True,
+                    stop=True,
+                )
+            for t in range(PACK):
+                nc.scalar.activation(size_window[t][:, lo:hi], parts[t], ACT.Abs)
+            for t in range(PACK):
+                nc.scalar.copy(h_window[t][:, lo:hi], parts[t])
+            for b in banks:
+                members = [m for m in range(PACK) if h_banks[c][m] == b]
+                nc.scalar.activation(size_plain[:, members[0] : members[-1] + 1, lo:hi], banks[b][:], ACT.Abs)
+
+        gather_sum(0)
+        for u in range(len(units)):
+            if u + 1 < len(units):
+                gather_sum(u + 1)
+            if u >= 1:
+                larger_gap(u - 1)
+            if u >= 2 and units[u - 2][1] == PACK - 1:
+                second_product(units[u - 2][0])
+            gather_gaps(u)
+        larger_gap(len(units) - 1)
+        second_product(len(PIECES_Z) - 1)
+
+        out_rows = out_0.rearrange("(p t) n -> p t n", t=PACK)
+        out_words_dram = out_1[0].rearrange("p n r -> p (n r)").bitcast(I32)
+        out_words = held([P, S], U32, "out_words")
+        out_scale = held([P, S], U8, "out_scale")
+        result = [held([P, PACK, hi - lo], F32, f"result{lo}") for lo, hi in PIECES_OUT]
+        result_grouped = [held([P, hi - lo, PACK], BF16, f"result_grouped{lo}") for lo, hi in PIECES_OUT]
+        out_units = [(c, t) for c in range(len(PIECES_OUT)) for t in range(PACK)]
+        inverse = {}
+
+        def denominator(u):
+            c, t = out_units[u]
+            lo, hi = PIECES_OUT[c]
+            den = ring.tile([P, hi - lo], F32, tag="den", name=f"den{u}")
+            nc.vector.tensor_tensor(
+                den[:], size_window[t][:].indirect(entries(n5_sb, lo, hi)), size_plain[:, t, lo:hi], ALU.add
+            )
+            root = ring.tile([P, hi - lo], F32, tag="root", name=f"root{u}")
+            nc.scalar.activation(root[:], den[:], ACT.Abs_reciprocal_sqrt, bias=half[:])
+            inverse[u] = ring.tile([P, hi - lo], F32, tag="inverse", name=f"inverse{u}", bufs=6)
+            nc.scalar.activation(inverse[u][:], root[:], ACT.Square)
+
+        def quotient(u):
+            c, t = out_units[u]
+            lo, hi = PIECES_OUT[c]
+            nc.vector.tensor_tensor(
+                result[c][:, t, :], h_window[t][:].indirect(entries(n4_sb, lo, hi)), inverse[u][:], ALU.mult
+            )
+
+        def hand_out(c):
+            lo, hi = PIECES_OUT[c]
+            nc.sync.dma_start(out_rows[:, :, lo:hi], result[c][:])
+            woven = result[c][:].rearrange("p t n -> p n t")
+            if c + 1 < len(PIECES_OUT):
+                nc.scalar.copy(result_grouped[c][:], woven)
+            else:
+                nc.vector.tensor_copy(result_grouped[c][:], woven)
+
+        def quantise_out(c):
+            lo, hi = PIECES_OUT[c]
+            nc.vector.quantize_mx(
+                out=out_words[:, lo:hi].bitcast(FP8X4),
+                scales=out_scale[:, lo:hi],
+                in_=result_grouped[c][:].rearrange("p n t -> p (n t)"),
+            )
+            nc.sync.dma_start(out_words_dram[:, lo:hi], out_words[:, lo:hi].bitcast(I32))
+
+        lag = 3
+        for u in range(len(out_units) + lag):
+            if u < len(out_units):
+                denominator(u)
+            v = u - lag
+            if v >= 0:
+                quotient(v)
+                if out_units[v][1] == PACK - 1:
+                    hand_out(out_units[v][0])
+                if out_units[v][1] == PACK - 1 and out_units[v][0] >= 1:
+                    quantise_out(out_units[v][0] - 1)
+        quantise_out(len(PIECES_OUT) - 1)
+        scale_rows = out_2[0].bitcast(I32)
+        for q in range(4):
+            queue = nc.scalar if q % 2 else nc.sync
+            queue.dma_start(scale_rows[4 * q : 4 * q + 4, :], out_scale[:].bitcast(I32)[32 * q : 32 * q + 4, :])

@@ -18,8 +18,6 @@ ACT = mybir.ActivationFunctionType
 
 P = 128
 PACK = 4
-PIECES_Z = ((0, 256), (256, 384), (384, 512))
-PIECES_OUT = ((0, 256), (256, 384), (384, 512))
 
 
 def tile_picked_keytrimnorm2_none_po_kernel(
@@ -30,6 +28,7 @@ def tile_picked_keytrimnorm2_none_po_kernel(
     with ExitStack() as ctx:
         keep = ctx.enter_context(tc.tile_pool(name="keep", bufs=1))
         ring = ctx.enter_context(tc.tile_pool(name="ring", bufs=4))
+        overlay = ctx.enter_context(tc.tile_pool(name="overlay", bufs=1))
         psum = ctx.enter_context(tc.psum_pool(name="psum", bufs=1))
 
         def held(shape, dtype, name):
@@ -46,7 +45,7 @@ def tile_picked_keytrimnorm2_none_po_kernel(
         d_bytes = held([P, G], U8, "d_bytes")
         x_bytes = held([P, T], U8, "x_bytes")
         w_bytes = held([P, N], U8, "w_bytes")
-        nc.vector.memset(d_bytes[:].bitcast(I32), 0)
+        nc.gpsimd.memset(d_bytes[:].bitcast(I32), 0)
         nc.vector.memset(x_bytes[:].bitcast(I32), 0)
         nc.gpsimd.memset(w_bytes[:].bitcast(I32), 0)
         four = held([P, 1], F32, "four")
@@ -57,64 +56,60 @@ def tile_picked_keytrimnorm2_none_po_kernel(
         offs_sb = load_list(offs, "offs_sb")
         x_rows = x_scales[0].bitcast(I32)
         for q in range(4):
-            nc.scalar.dma_start(x_bytes[:].bitcast(I32)[32 * q : 32 * q + 4, :], x_rows[4 * q : 4 * q + 4, :])
+            nc.sync.dma_start(x_bytes[:].bitcast(I32)[32 * q : 32 * q + 4, :], x_rows[4 * q : 4 * q + 4, :])
         half = held([P, 1], F32, "half")
         nc.scalar.activation(half[:], four[:], ACT.Abs_reciprocal_sqrt)
         d_table = held([P, G], U32, "d_table")
         nc.sync.dma_start(d_table[:].bitcast(I32), d_words[0].rearrange("p n r -> p (n r)").bitcast(I32))
-        x_table = held([P, T], U32, "x_table")
+        x_table = overlay.tile([P, T], U32, name="x_table", offset=2048, align_bytes=64)
         nc.sync.dma_start(x_table[:].bitcast(I32), x_words[0].rearrange("p n r -> p (n r)").bitcast(I32))
+        w_table = held([P, 2 * N], U8, "w_table")
+        nc.gpsimd.dma_start(w_table[:].bitcast(I32), w1_words[0].bitcast(I32))
+        w_rows = w1_scales[0].bitcast(I32)
+        for q in range(4):
+            nc.gpsimd.dma_start(w_bytes[:].bitcast(I32)[32 * q : 32 * q + 4, :], w_rows[4 * q : 4 * q + 4, :])
         n1_sb = load_list(n1, "n1_sb")
         n2_sb = load_list(n2, "n2_sb")
         n3_sb = load_list(n3, "n3_sb")
         gain = held([P, PACK], F32, "gain")
-        nc.sync.dma_start(gain[:], gn.rearrange("(p t) o -> p (t o)", t=PACK))
-        w_table = held([P, 2 * N], U8, "w_table")
-        nc.sync.dma_start(w_table[:].bitcast(I32), w1_words[0].bitcast(I32))
-        w_rows = w1_scales[0].bitcast(I32)
-        for q in range(4):
-            nc.sync.dma_start(w_bytes[:].bitcast(I32)[32 * q : 32 * q + 4, :], w_rows[4 * q : 4 * q + 4, :])
+        nc.gpsimd.dma_start(gain[:], gn.rearrange("(p t) o -> p (t o)", t=PACK))
         n5_sb = load_list(n5, "n5_sb")
         n4_sb = load_list(n4, "n4_sb")
 
         key_bytes = held([P, H], U8, "key_bytes")
         nc.vector.tensor_copy(key_bytes[:], d_bytes[:].indirect(kidx_sb[:]))
-        key_bytes_dealt = held([P, H], U8, "key_bytes_dealt")
+        key_scale = held([P, H], U8, "key_scale")
         nc.vector.tensor_copy(
-            key_bytes_dealt[:].rearrange("p (t m) -> p t m", t=PACK),
+            key_scale[:].rearrange("p (t m) -> p t m", t=PACK),
             key_bytes[:].rearrange("p (m t) -> p t m", t=PACK),
         )
-        key_scale = held([P, H], U8, "key_scale")
-        nc.vector.tensor_copy(key_scale[:].bitcast(I32), key_bytes_dealt[:].bitcast(I32))
         for r in range(1, 4):
-            nc.scalar.dma_start(
-                key_scale[:].bitcast(I32)[r:P:32, :], key_bytes_dealt[:].bitcast(I32)[8 * r : P : 32, :]
-            )
+            nc.scalar.dma_start(key_scale[:].bitcast(I32)[r:P:32, :], key_scale[:].bitcast(I32)[8 * r : P : 32, :])
         query_scale = held([P, S], U8, "query_scale")
         nc.vector.tensor_copy(query_scale[:], x_bytes[:].indirect(offs_sb[:]))
         key_words = held([P, H], U32, "key_words")
         nc.vector.tensor_copy(key_words[:], d_table[:].indirect(kidx_sb[:]))
         key_dealt = held([P, H], U32, "key_dealt")
         nc.vector.tensor_copy(
-            key_dealt[:].bitcast(I32).rearrange("p (t m) -> p t m", t=PACK),
-            key_words[:].bitcast(I32).rearrange("p (m t) -> p t m", t=PACK),
+            key_dealt[:].bitcast(I32).rearrange("p (t m) -> p m t", t=PACK),
+            key_words[:].bitcast(I32).rearrange("p (m t) -> p m t", t=PACK),
         )
         query_words = held([P, S], U32, "query_words")
         for lo, hi in ((0, 256), (256, 512)):
             nc.vector.tensor_copy(query_words[:, lo:hi], x_table[:].indirect(entries(offs_sb, lo, hi)))
 
-        w_dealt = held([P, 2 * N], U8, "w_dealt")
+        w_dealt = overlay.tile([P, 2 * N], U8, name="w_dealt", offset=2048, align_bytes=64)
         nc.vector.tensor_copy(
             w_dealt[:].rearrange("p (t m b) -> p t m b", t=PACK, b=2),
             w_table[:].rearrange("p (m t b) -> p t m b", t=PACK, b=2),
         )
         w_scale = held([P, N], U8, "w_scale")
-        nc.vector.tensor_copy(
+        nc.gpsimd.tensor_copy(
             w_scale[:].rearrange("p (t m) -> p t m", t=PACK),
             w_bytes[:].rearrange("p (m t) -> p t m", t=PACK),
         )
         factor = held([P, PACK], F32, "factor")
-        nc.scalar.activation(factor[:], gain[:], ACT.Copy, scale=-0.0625)
+        nc.gpsimd.tensor_scalar(factor[:], gain[:], -0.0625, 0.0, ALU.mult, ALU.add)
 
         def score_matmul(bank, t, lo, hi):
             acc = psum.tile([P, hi - lo], F32, tag=f"bank{bank}", name=f"score{t}_{lo}")
@@ -130,7 +125,9 @@ def tile_picked_keytrimnorm2_none_po_kernel(
             return acc
 
         score = [held([P, S], F32, f"score_window{t}") for t in range(PACK)]
-        score_plain = [held([P, S], F32, f"score_plain{t}") for t in range(PACK)]
+        h_window = [held([P, S if t < 2 else 2 * S], F32, f"h_window{t}") for t in range(PACK)]
+        size_window = [held([P, S if t < 2 else 2 * S], F32, f"size_window{t}") for t in range(PACK)]
+        score_plain = [w[:, S : 2 * S] for w in (size_window[2], size_window[3], h_window[2], h_window[3])]
         first = score_matmul(0, 0, 0, 256)
         second = score_matmul(1, 0, 256, 512)
         rest = [score_matmul(1 + t, t, 0, S) for t in range(1, PACK)]
@@ -144,61 +141,57 @@ def tile_picked_keytrimnorm2_none_po_kernel(
         for t in range(1, PACK):
             nc.scalar.copy(score_plain[t][:, 256:512], rest[t - 1][:, 256:512])
 
-        h_window = [held([P, S], F32, f"h_window{t}") for t in range(PACK)]
-        size_window = [held([P, S], F32, f"size_window{t}") for t in range(PACK)]
         size_plain = held([P, PACK, S], F32, "size_plain")
         z_words = held([P, S], U32, "z_words")
         z_scale = held([P, S], U8, "z_scale")
-        z_grouped = [held([P, hi - lo, PACK], BF16, f"z_grouped{lo}") for lo, hi in PIECES_Z]
-        h_banks = ((5, 5, 6, 6), (7, 7, 7, 7), (0, 1, 2, 3))
+        z_first = overlay.tile([P, 256, PACK], BF16, name="z_first", offset=0, align_bytes=64)
+        z_second = held([P, 256, PACK], BF16, "z_second")
 
-        units = [(c, t) for c in range(len(PIECES_Z)) for t in range(PACK)]
+        units = [(t, 0, 256) for t in range(PACK)] + [(t, 256, 512) for t in range(PACK - 1)]
+        units = units + [(PACK - 1, 256, 384), (PACK - 1, 384, 512)]
         sums = {}
         gaps = {}
 
         def gather_sum(u):
-            c, t = units[u]
-            lo, hi = PIECES_Z[c]
+            t, lo, hi = units[u]
             sums[u] = ring.tile([P, hi - lo], F32, tag="sum", name=f"sum{u}")
             nc.vector.tensor_tensor(
                 sums[u][:], score[t][:].indirect(entries(n1_sb, lo, hi)), score_plain[t][:, lo:hi], ALU.add
             )
 
         def gather_gaps(u):
-            c, t = units[u]
-            lo, hi = PIECES_Z[c]
+            t, lo, hi = units[u]
             gaps[u] = []
-            for name, lst in (("gap2", n2_sb), ("gap3", n3_sb)):
-                gap = ring.tile([P, hi - lo], F32, tag=name, name=f"{name}_{u}")
+            for i, lst in enumerate((n2_sb, n3_sb)):
+                if u == 5:
+                    gap = overlay.tile([P, hi - lo], F32, name=f"gap{i}_{u}", offset=1024 * i, align_bytes=64)
+                else:
+                    gap = ring.tile([P, hi - lo], F32, tag=f"gap{i}", name=f"gap{i}_{u}")
                 nc.vector.tensor_tensor(gap[:], score[t][:].indirect(entries(lst, lo, hi)), sums[u][:], ALU.subtract)
                 gaps[u].append(gap)
 
         def larger_gap(u):
-            c, t = units[u]
-            lo, hi = PIECES_Z[c]
+            t, lo, hi = units[u]
             larger = ring.tile([P, hi - lo], F32, tag="larger", name=f"larger{u}")
             nc.vector.tensor_tensor(larger[:], gaps[u][0][:], gaps[u][1][:], ALU.max)
-            nc.scalar.activation(z_grouped[c][:, :, t], larger[:], ACT.Copy, scale=factor[:, t : t + 1])
+            if lo < 256:
+                nc.scalar.activation(z_first[:, :, t], larger[:, 0:256], ACT.Copy, scale=factor[:, t : t + 1])
+            if hi > 256:
+                start = max(lo, 256)
+                nc.scalar.activation(
+                    z_second[:, start - 256 : hi - 256, t], larger[:, start - lo : hi - lo], ACT.Copy,
+                    scale=factor[:, t : t + 1],
+                )
 
-        def second_product(c):
-            lo, hi = PIECES_Z[c]
-            w = hi - lo
+        def second_product(source, lo, hi, parts):
             nc.vector.quantize_mx(
                 out=z_words[:, lo:hi].bitcast(FP8X4),
                 scales=z_scale[:, lo:hi],
-                in_=z_grouped[c][:].rearrange("p n t -> p (n t)"),
+                in_=source.rearrange("p n t -> p (n t)"),
             )
-            banks = {}
-            parts = []
             for t in range(PACK):
-                b = h_banks[c][t]
-                members = [m for m in range(PACK) if h_banks[c][m] == b]
-                if b not in banks:
-                    banks[b] = psum.tile([P, len(members), w], F32, tag=f"bank{b}", name=f"h{c}_{b}")
-                part = banks[b][:, t - members[0], :]
-                parts.append(part)
                 nc.tensor.matmul_mx(
-                    out=part,
+                    out=parts[t],
                     lhsT=w_dealt[:, 2 * t * P : 2 * (t + 1) * P].bitcast(FP4X4),
                     lhsT_scale=w_scale[:, t * P : (t + 1) * P],
                     rhs=z_words[:, lo:hi].bitcast(FP8X4),
@@ -206,38 +199,60 @@ def tile_picked_keytrimnorm2_none_po_kernel(
                     start=True,
                     stop=True,
                 )
-            for t in range(PACK):
-                nc.scalar.activation(size_window[t][:, lo:hi], parts[t], ACT.Abs)
-            for t in range(PACK):
-                nc.scalar.copy(h_window[t][:, lo:hi], parts[t])
-            for b in banks:
-                members = [m for m in range(PACK) if h_banks[c][m] == b]
-                nc.scalar.activation(size_plain[:, members[0] : members[-1] + 1, lo:hi], banks[b][:], ACT.Abs)
 
         gather_sum(0)
         for u in range(len(units)):
+            if u == 5:
+                pair = [psum.tile([P, 2, 256], F32, tag=f"bank{5 + i}", name=f"h_first{i}") for i in range(2)]
+                h_first = [pair[t // 2][:, t % 2, :] for t in range(PACK)]
+                second_product(z_first[:], 0, 256, h_first)
             if u + 1 < len(units):
                 gather_sum(u + 1)
             if u >= 1:
                 larger_gap(u - 1)
-            if u >= 2 and units[u - 2][1] == PACK - 1:
-                second_product(units[u - 2][0])
+            if u == 5:
+                for t in range(PACK):
+                    nc.scalar.activation(size_window[t][:, 0:256], h_first[t], ACT.Abs)
+            if u == 6:
+                for i in range(2):
+                    nc.scalar.activation(size_plain[:, 2 * i : 2 * i + 2, 0:256], pair[i][:], ACT.Abs)
+            if u == 7:
+                for t in range(PACK):
+                    nc.scalar.copy(h_window[t][:, 0:256], h_first[t])
             gather_gaps(u)
         larger_gap(len(units) - 1)
-        second_product(len(PIECES_Z) - 1)
+
+        lone = psum.tile([P, 128], F32, tag="bank7", name="h_lone")
+        last = psum.tile([P, 128], F32, tag="bank0", name="h_last")
+        both = [psum.tile([P, 256], F32, tag=f"bank{t}", name=f"h_both{t}") for t in range(1, PACK)]
+        second_product(z_second[:, 0:128, :], 256, 384, [lone[:]] + [b[:, 0:128] for b in both])
+        nc.scalar.activation(size_window[0][:, 256:384], lone[:], ACT.Abs)
+        second_product(z_second[:, 128:256, :], 384, 512, [last[:]] + [b[:, 128:256] for b in both])
+        nc.scalar.activation(size_window[0][:, 384:512], last[:], ACT.Abs)
+        for t in range(1, PACK):
+            nc.scalar.activation(size_window[t][:, 256:512], both[t - 1][:], ACT.Abs)
+
+        def late_copies(t):
+            if t == 0:
+                nc.scalar.copy(h_window[0][:, 256:384], lone[:])
+                nc.scalar.copy(h_window[0][:, 384:512], last[:])
+                nc.scalar.activation(size_plain[:, 0, 256:384], lone[:], ACT.Abs)
+                nc.scalar.activation(size_plain[:, 0, 384:512], last[:], ACT.Abs)
+            else:
+                nc.scalar.copy(h_window[t][:, 256:512], both[t - 1][:])
+                nc.scalar.activation(size_plain[:, t, 256:512], both[t - 1][:], ACT.Abs)
 
         out_rows = out_0.rearrange("(p t) n -> p t n", t=PACK)
         out_words_dram = out_1[0].rearrange("p n r -> p (n r)").bitcast(I32)
         out_words = held([P, S], U32, "out_words")
         out_scale = held([P, S], U8, "out_scale")
-        result = [held([P, PACK, hi - lo], F32, f"result{lo}") for lo, hi in PIECES_OUT]
-        result_grouped = [held([P, hi - lo, PACK], BF16, f"result_grouped{lo}") for lo, hi in PIECES_OUT]
-        out_units = [(c, t) for c in range(len(PIECES_OUT)) for t in range(PACK)]
+        result = held([P, PACK, S], F32, "result")
+        grouped = [held([P, 256, PACK], BF16, f"grouped{c}") for c in range(2)]
+        out_units = [(0, 0, 256), (1, 0, 256), (2, 0, 512), (3, 0, 512), (0, 256, 512), (1, 256, 512)]
         inverse = {}
 
         def denominator(u):
-            c, t = out_units[u]
-            lo, hi = PIECES_OUT[c]
+            t, lo, hi = out_units[u]
             den = ring.tile([P, hi - lo], F32, tag="den", name=f"den{u}")
             nc.vector.tensor_tensor(
                 den[:], size_window[t][:].indirect(entries(n5_sb, lo, hi)), size_plain[:, t, lo:hi], ALU.add
@@ -248,42 +263,43 @@ def tile_picked_keytrimnorm2_none_po_kernel(
             nc.scalar.activation(inverse[u][:], root[:], ACT.Square)
 
         def quotient(u):
-            c, t = out_units[u]
-            lo, hi = PIECES_OUT[c]
+            t, lo, hi = out_units[u]
             nc.vector.tensor_tensor(
-                result[c][:, t, :], h_window[t][:].indirect(entries(n4_sb, lo, hi)), inverse[u][:], ALU.mult
+                result[:, t, lo:hi], h_window[t][:].indirect(entries(n4_sb, lo, hi)), inverse[u][:], ALU.mult
             )
-
-        def hand_out(c):
-            lo, hi = PIECES_OUT[c]
-            nc.sync.dma_start(out_rows[:, :, lo:hi], result[c][:])
-            woven = result[c][:].rearrange("p t n -> p n t")
-            if c + 1 < len(PIECES_OUT):
-                nc.scalar.copy(result_grouped[c][:], woven)
-            else:
-                nc.vector.tensor_copy(result_grouped[c][:], woven)
+            nc.sync.dma_start(out_rows[:, t, lo:hi], result[:, t, lo:hi])
 
         def quantise_out(c):
-            lo, hi = PIECES_OUT[c]
+            lo, hi = 256 * c, 256 * (c + 1)
             nc.vector.quantize_mx(
                 out=out_words[:, lo:hi].bitcast(FP8X4),
                 scales=out_scale[:, lo:hi],
-                in_=result_grouped[c][:].rearrange("p n t -> p (n t)"),
+                in_=grouped[c][:].rearrange("p n t -> p (n t)"),
             )
             nc.sync.dma_start(out_words_dram[:, lo:hi], out_words[:, lo:hi].bitcast(I32))
 
-        lag = 3
-        for u in range(len(out_units) + lag):
-            if u < len(out_units):
-                denominator(u)
-            v = u - lag
-            if v >= 0:
-                quotient(v)
-                if out_units[v][1] == PACK - 1:
-                    hand_out(out_units[v][0])
-                if out_units[v][1] == PACK - 1 and out_units[v][0] >= 1:
-                    quantise_out(out_units[v][0] - 1)
-        quantise_out(len(PIECES_OUT) - 1)
+        woven = result[:].rearrange("p t n -> p n t")
+        denominator(0)
+        late_copies(0)
+        denominator(1)
+        late_copies(2)
+        denominator(2)
+        late_copies(1)
+        quotient(0)
+        late_copies(3)
+        denominator(3)
+        quotient(1)
+        quotient(2)
+        denominator(4)
+        quotient(3)
+        nc.scalar.copy(grouped[0][:], woven[:, 0:256, :])
+        denominator(5)
+        quotient(4)
+        quotient(5)
+        quantise_out(0)
+        nc.vector.tensor_copy(grouped[1][:, 0:160, :], woven[:, 256:416, :])
+        nc.scalar.copy(grouped[1][:, 160:256, :], woven[:, 416:512, :])
+        quantise_out(1)
         scale_rows = out_2[0].bitcast(I32)
         for q in range(4):
             queue = nc.scalar if q % 2 else nc.sync

@@ -124,7 +124,8 @@ def tile_picked_keytrimnorm2_none_po_kernel(
             )
             return acc
 
-        score = [held([P, S], F32, f"score_window{t}") for t in range(PACK)]
+        score = [held([P, 2 * S if t == 0 else S], F32, f"score_window{t}") for t in range(PACK)]
+        nc.scalar.copy(score[0][:, S : 2 * S], half[:].to_broadcast([P, S]))
         h_window = [held([P, S if t < 2 else 2 * S], F32, f"h_window{t}") for t in range(PACK)]
         size_window = [held([P, S if t < 2 else 2 * S], F32, f"size_window{t}") for t in range(PACK)]
         score_plain = [w[:, S : 2 * S] for w in (size_window[2], size_window[3], h_window[2], h_window[3])]
@@ -134,20 +135,20 @@ def tile_picked_keytrimnorm2_none_po_kernel(
         nc.scalar.copy(score[0][:, 0:256], first[:])
         nc.scalar.copy(score_plain[0][:, 0:256], first[:])
         nc.scalar.copy(score[0][:, 256:512], second[:])
+        nc.scalar.copy(score_plain[0][:, 256:512], second[:])
         for t in range(1, PACK):
             nc.scalar.copy(score[t][:], rest[t - 1][:])
             nc.scalar.copy(score_plain[t][:, 0:256], rest[t - 1][:, 0:256])
-        nc.scalar.copy(score_plain[0][:, 256:512], second[:])
         for t in range(1, PACK):
             nc.scalar.copy(score_plain[t][:, 256:512], rest[t - 1][:, 256:512])
 
-        size_plain = held([P, PACK, S], F32, "size_plain")
+        size_plain = [held([P, S], F32, f"size_plain{t}") for t in range(PACK)]
         z_words = held([P, S], U32, "z_words")
         z_scale = held([P, S], U8, "z_scale")
         z_first = overlay.tile([P, 256, PACK], BF16, name="z_first", offset=0, align_bytes=64)
         z_second = held([P, 256, PACK], BF16, "z_second")
 
-        units = [(t, 0, 256) for t in range(PACK)] + [(t, 256, 512) for t in range(PACK - 1)]
+        units = [(0, 0, 512)] + [(t, 0, 256) for t in range(1, PACK)] + [(t, 256, 512) for t in range(1, PACK - 1)]
         units = units + [(PACK - 1, 256, 384), (PACK - 1, 384, 512)]
         sums = {}
         gaps = {}
@@ -213,14 +214,14 @@ def tile_picked_keytrimnorm2_none_po_kernel(
             if u == 5:
                 for t in range(PACK):
                     nc.scalar.activation(size_window[t][:, 0:256], h_first[t], ACT.Abs)
+                    nc.sync.dma_start(size_plain[t][:, 0:256], size_window[t][:, 0:256])
             if u == 6:
-                for i in range(2):
-                    nc.scalar.activation(size_plain[:, 2 * i : 2 * i + 2, 0:256], pair[i][:], ACT.Abs)
-            if u == 7:
-                for t in range(PACK):
+                for t in range(2):
                     nc.scalar.copy(h_window[t][:, 0:256], h_first[t])
             gather_gaps(u)
         larger_gap(len(units) - 1)
+        for t in range(2, PACK):
+            nc.scalar.copy(h_window[t][:, 0:256], h_first[t])
 
         lone = psum.tile([P, 128], F32, tag="bank7", name="h_lone")
         last = psum.tile([P, 128], F32, tag="bank0", name="h_last")
@@ -231,16 +232,18 @@ def tile_picked_keytrimnorm2_none_po_kernel(
         nc.scalar.activation(size_window[0][:, 384:512], last[:], ACT.Abs)
         for t in range(1, PACK):
             nc.scalar.activation(size_window[t][:, 256:512], both[t - 1][:], ACT.Abs)
+        for t in range(2):
+            nc.sync.dma_start(size_plain[t][:, 256:512], size_window[t][:, 256:512])
 
         def late_copies(t):
             if t == 0:
                 nc.scalar.copy(h_window[0][:, 256:384], lone[:])
                 nc.scalar.copy(h_window[0][:, 384:512], last[:])
-                nc.scalar.activation(size_plain[:, 0, 256:384], lone[:], ACT.Abs)
-                nc.scalar.activation(size_plain[:, 0, 384:512], last[:], ACT.Abs)
             else:
                 nc.scalar.copy(h_window[t][:, 256:512], both[t - 1][:])
-                nc.scalar.activation(size_plain[:, t, 256:512], both[t - 1][:], ACT.Abs)
+
+        def late_sizes(t):
+            nc.scalar.activation(size_plain[t][:, 256:512], both[t - 1][:], ACT.Abs)
 
         out_rows = out_0.rearrange("(p t) n -> p t n", t=PACK)
         out_words_dram = out_1[0].rearrange("p n r -> p (n r)").bitcast(I32)
@@ -255,7 +258,7 @@ def tile_picked_keytrimnorm2_none_po_kernel(
             t, lo, hi = out_units[u]
             den = ring.tile([P, hi - lo], F32, tag="den", name=f"den{u}")
             nc.vector.tensor_tensor(
-                den[:], size_window[t][:].indirect(entries(n5_sb, lo, hi)), size_plain[:, t, lo:hi], ALU.add
+                den[:], size_window[t][:].indirect(entries(n5_sb, lo, hi)), size_plain[t][:, lo:hi], ALU.add
             )
             root = ring.tile([P, hi - lo], F32, tag="root", name=f"root{u}")
             nc.scalar.activation(root[:], den[:], ACT.Abs_reciprocal_sqrt, bias=half[:])
@@ -279,15 +282,17 @@ def tile_picked_keytrimnorm2_none_po_kernel(
             nc.sync.dma_start(out_words_dram[:, lo:hi], out_words[:, lo:hi].bitcast(I32))
 
         woven = result[:].rearrange("p t n -> p n t")
+        late_sizes(2)
         denominator(0)
         late_copies(0)
         denominator(1)
-        late_copies(2)
-        denominator(2)
+        late_sizes(3)
         late_copies(1)
+        denominator(2)
         quotient(0)
-        late_copies(3)
+        late_copies(2)
         denominator(3)
+        late_copies(3)
         quotient(1)
         quotient(2)
         denominator(4)

@@ -89,15 +89,18 @@ def tile_picked_keytrimnorm2_none_po_kernel(
         nc.vector.tensor_copy(query_scale[:], x_bytes[:].indirect(offs_sb[:]))
         key_words = held([P, H], U32, "key_words")
         nc.vector.tensor_copy(key_words[:], d_table[:].indirect(kidx_sb[:]))
-        key_dealt = held([P, H], U32, "key_dealt")
-        nc.vector.tensor_copy(
-            key_dealt[:].bitcast(I32).rearrange("p (t m) -> p m t", t=PACK),
-            key_words[:].bitcast(I32).rearrange("p (m t) -> p m t", t=PACK),
-        )
+        keys_by_slot = key_words[:].bitcast(I32).rearrange("p (m t) -> p m t", t=PACK)
+        key_first = held([P, P], U32, "key_first")
+        nc.vector.tensor_copy(key_first[:].bitcast(I32), keys_by_slot[:, :, 0])
         query_words = held([P, S], U32, "query_words")
         for lo, hi in ((0, 256), (256, 512)):
             nc.vector.tensor_copy(query_words[:, lo:hi], x_table[:].indirect(entries(offs_sb, lo, hi)))
 
+        key_rest = overlay.tile([P, 3 * P], U32, name="key_rest", offset=4096, align_bytes=64)
+        nc.vector.tensor_copy(
+            key_rest[:].bitcast(I32).rearrange("p (t m) -> p m t", t=PACK - 1), keys_by_slot[:, :, 1:PACK]
+        )
+        key_dealt = [key_first[:]] + [key_rest[:, t * P : (t + 1) * P] for t in range(PACK - 1)]
         w_dealt = overlay.tile([P, 2 * N], U8, name="w_dealt", offset=2048, align_bytes=64)
         nc.vector.tensor_copy(
             w_dealt[:].rearrange("p (t m b) -> p t m b", t=PACK, b=2),
@@ -115,7 +118,7 @@ def tile_picked_keytrimnorm2_none_po_kernel(
             acc = psum.tile([P, hi - lo], F32, tag=f"bank{bank}", name=f"score{t}_{lo}")
             nc.tensor.matmul_mx(
                 out=acc[:],
-                lhsT=key_dealt[:, t * P : (t + 1) * P].bitcast(FP8X4),
+                lhsT=key_dealt[t].bitcast(FP8X4),
                 lhsT_scale=key_scale[:, t * P : (t + 1) * P],
                 rhs=query_words[:, lo:hi].bitcast(FP8X4),
                 rhs_scale=query_scale[:, lo:hi],
@@ -124,11 +127,12 @@ def tile_picked_keytrimnorm2_none_po_kernel(
             )
             return acc
 
-        score = [held([P, 2 * S if t == 0 else S], F32, f"score_window{t}") for t in range(PACK)]
-        nc.scalar.copy(score[0][:, S : 2 * S], half[:].to_broadcast([P, S]))
+        score = [held([P, 2 * S if t < 2 else S], F32, f"score_window{t}") for t in range(PACK)]
         h_window = [held([P, S if t < 2 else 2 * S], F32, f"h_window{t}") for t in range(PACK)]
         size_window = [held([P, S if t < 2 else 2 * S], F32, f"size_window{t}") for t in range(PACK)]
-        score_plain = [w[:, S : 2 * S] for w in (size_window[2], size_window[3], h_window[2], h_window[3])]
+        score_plain = [w[:, S : 2 * S] for w in (score[1], size_window[2], size_window[3], h_window[2])]
+        for w in (score[0], h_window[3]):
+            nc.scalar.copy(w[:, S : 2 * S], half[:].to_broadcast([P, S]))
         first = score_matmul(0, 0, 0, 256)
         second = score_matmul(1, 0, 256, 512)
         rest = [score_matmul(1 + t, t, 0, S) for t in range(1, PACK)]
@@ -137,10 +141,8 @@ def tile_picked_keytrimnorm2_none_po_kernel(
         nc.scalar.copy(score[0][:, 256:512], second[:])
         nc.scalar.copy(score_plain[0][:, 256:512], second[:])
         for t in range(1, PACK):
-            nc.scalar.copy(score[t][:], rest[t - 1][:])
-            nc.scalar.copy(score_plain[t][:, 0:256], rest[t - 1][:, 0:256])
-        for t in range(1, PACK):
-            nc.scalar.copy(score_plain[t][:, 256:512], rest[t - 1][:, 256:512])
+            nc.scalar.copy(score[t][:, 0:S], rest[t - 1][:])
+            nc.scalar.copy(score_plain[t], rest[t - 1][:])
 
         size_plain = [held([P, S], F32, f"size_plain{t}") for t in range(PACK)]
         z_words = held([P, S], U32, "z_words")
@@ -148,16 +150,18 @@ def tile_picked_keytrimnorm2_none_po_kernel(
         z_first = overlay.tile([P, 256, PACK], BF16, name="z_first", offset=0, align_bytes=64)
         z_second = held([P, 256, PACK], BF16, "z_second")
 
-        units = [(0, 0, 512)] + [(t, 0, 256) for t in range(1, PACK)] + [(t, 256, 512) for t in range(1, PACK - 1)]
-        units = units + [(PACK - 1, 256, 384), (PACK - 1, 384, 512)]
+        units = [(0, 0, 512), (1, 0, 512), (2, 0, 256), (3, 0, 256), (2, 256, 512), (3, 256, 384), (3, 384, 512)]
         sums = {}
         gaps = {}
 
         def gather_sum(u):
             t, lo, hi = units[u]
-            sums[u] = ring.tile([P, hi - lo], F32, tag="sum", name=f"sum{u}")
+            if u == 6:
+                sums[u] = h_window[3][:, 0:128]
+            else:
+                sums[u] = ring.tile([P, hi - lo], F32, tag="sum", name=f"sum{u}")[:]
             nc.vector.tensor_tensor(
-                sums[u][:], score[t][:].indirect(entries(n1_sb, lo, hi)), score_plain[t][:, lo:hi], ALU.add
+                sums[u], score[t][:].indirect(entries(n1_sb, lo, hi)), score_plain[t][:, lo:hi], ALU.add
             )
 
         def gather_gaps(u):
@@ -165,16 +169,21 @@ def tile_picked_keytrimnorm2_none_po_kernel(
             gaps[u] = []
             for i, lst in enumerate((n2_sb, n3_sb)):
                 if u == 5:
-                    gap = overlay.tile([P, hi - lo], F32, name=f"gap{i}_{u}", offset=1024 * i, align_bytes=64)
+                    gap = overlay.tile([P, hi - lo], F32, name=f"gap{i}_{u}", offset=1024 * i, align_bytes=64)[:]
+                elif u == 6:
+                    gap = h_window[i][:, 0:128]
                 else:
-                    gap = ring.tile([P, hi - lo], F32, tag=f"gap{i}", name=f"gap{i}_{u}")
-                nc.vector.tensor_tensor(gap[:], score[t][:].indirect(entries(lst, lo, hi)), sums[u][:], ALU.subtract)
+                    gap = ring.tile([P, hi - lo], F32, tag=f"gap{i}", name=f"gap{i}_{u}")[:]
+                nc.vector.tensor_tensor(gap, score[t][:].indirect(entries(lst, lo, hi)), sums[u], ALU.subtract)
                 gaps[u].append(gap)
 
         def larger_gap(u):
             t, lo, hi = units[u]
-            larger = ring.tile([P, hi - lo], F32, tag="larger", name=f"larger{u}")
-            nc.vector.tensor_tensor(larger[:], gaps[u][0][:], gaps[u][1][:], ALU.max)
+            if u == 6:
+                larger = h_window[2][:, 0:128]
+            else:
+                larger = ring.tile([P, hi - lo], F32, tag="larger", name=f"larger{u}")[:]
+            nc.vector.tensor_tensor(larger, gaps[u][0], gaps[u][1], ALU.max)
             if lo < 256:
                 nc.scalar.activation(z_first[:, :, t], larger[:, 0:256], ACT.Copy, scale=factor[:, t : t + 1])
             if hi > 256:
@@ -201,6 +210,10 @@ def tile_picked_keytrimnorm2_none_po_kernel(
                     stop=True,
                 )
 
+        def first_sizes(t):
+            nc.scalar.activation(size_window[t][:, 0:256], h_first[t], ACT.Abs)
+            nc.sync.dma_start(size_plain[t][:, 0:256], size_window[t][:, 0:256])
+
         gather_sum(0)
         for u in range(len(units)):
             if u == 5:
@@ -212,24 +225,24 @@ def tile_picked_keytrimnorm2_none_po_kernel(
             if u >= 1:
                 larger_gap(u - 1)
             if u == 5:
-                for t in range(PACK):
-                    nc.scalar.activation(size_window[t][:, 0:256], h_first[t], ACT.Abs)
-                    nc.sync.dma_start(size_plain[t][:, 0:256], size_window[t][:, 0:256])
-            if u == 6:
-                for t in range(2):
-                    nc.scalar.copy(h_window[t][:, 0:256], h_first[t])
+                first_sizes(0)
+                first_sizes(1)
             gather_gaps(u)
+        nc.vector.tensor_copy(h_window[3][:, 0:256], h_first[3])
         larger_gap(len(units) - 1)
-        for t in range(2, PACK):
-            nc.scalar.copy(h_window[t][:, 0:256], h_first[t])
+        first_sizes(2)
+        first_sizes(3)
 
         lone = psum.tile([P, 128], F32, tag="bank7", name="h_lone")
         last = psum.tile([P, 128], F32, tag="bank0", name="h_last")
         both = [psum.tile([P, 256], F32, tag=f"bank{t}", name=f"h_both{t}") for t in range(1, PACK)]
         second_product(z_second[:, 0:128, :], 256, 384, [lone[:]] + [b[:, 0:128] for b in both])
         nc.scalar.activation(size_window[0][:, 256:384], lone[:], ACT.Abs)
+        for t in range(2):
+            nc.vector.tensor_copy(h_window[t][:, 0:256], h_first[t])
         second_product(z_second[:, 128:256, :], 384, 512, [last[:]] + [b[:, 128:256] for b in both])
         nc.scalar.activation(size_window[0][:, 384:512], last[:], ACT.Abs)
+        nc.vector.tensor_copy(h_window[2][:, 0:256], h_first[2])
         for t in range(1, PACK):
             nc.scalar.activation(size_window[t][:, 256:512], both[t - 1][:], ACT.Abs)
         for t in range(2):

@@ -64,7 +64,7 @@ def tile_picked_keytrimnorm2_none_po_kernel(
         x_table = overlay.tile([P, T], U32, name="x_table", offset=2048, align_bytes=64)
         nc.sync.dma_start(x_table[:].bitcast(I32), x_words[0].rearrange("p n r -> p (n r)").bitcast(I32))
         w_table = held([P, 2 * N], U8, "w_table")
-        nc.gpsimd.dma_start(w_table[:].bitcast(I32), w1_words[0].bitcast(I32))
+        nc.sync.dma_start(w_table[:].bitcast(I32), w1_words[0].bitcast(I32))
         w_rows = w1_scales[0].bitcast(I32)
         for q in range(4):
             nc.gpsimd.dma_start(w_bytes[:].bitcast(I32)[32 * q : 32 * q + 4, :], w_rows[4 * q : 4 * q + 4, :])

from contextlib import ExitStack

import concourse.mybir as mybir

K, T, S, N, G, H = 512, 2048, 512, 512, 2048, 512
FLOPS = 2 * K * H * S + 2 * H * N * S

F32 = mybir.dt.float32
BF16 = mybir.dt.bfloat16
I32 = mybir.dt.int32
U32 = mybir.dt.uint32
U16 = mybir.dt.uint16
U8 = mybir.dt.uint8
FP8X4 = mybir.dt.float8_e4m3fn_x4
FP4X4 = mybir.dt.float4_e2m1fn_x4
ALU = mybir.AluOpType
ACT = mybir.ActivationFunctionType

P = 128
PACK = 4


def tile_picked_keytrimnorm2_none_po_kernel(
    tc, x_words, x_scales, d_words, d_scales, gn, w1_words, w1_scales,
    offs, kidx, n1, n2, n3, n4, n5, out_0, out_1, out_2,
):
    nc = tc.nc
    with ExitStack() as ctx:
        keep = ctx.enter_context(tc.tile_pool(name="keep", bufs=1))
        ring = ctx.enter_context(tc.tile_pool(name="ring", bufs=4))
        overlay = ctx.enter_context(tc.tile_pool(name="overlay", bufs=1))
        psum = ctx.enter_context(tc.psum_pool(name="psum", bufs=1))

        def held(shape, dtype, name):
            return keep.tile(shape, dtype, name=name, align_bytes=64)

        def load_list(src, name):
            tile = keep.tile([P, S // 16], U16, name=name)
            nc.sync.dma_start(tile[:], src)
            return tile

        def entries(lst, lo, hi):
            return lst[:, lo // 16 : hi // 16]

        d_bytes = held([P, G], U8, "d_bytes")
        x_bytes = held([P, T], U8, "x_bytes")
        w_bytes = held([P, N], U8, "w_bytes")
        nc.gpsimd.memset(d_bytes[:].bitcast(I32), 0)
        nc.vector.memset(x_bytes[:].bitcast(I32), 0)
        nc.gpsimd.memset(w_bytes[:].bitcast(I32), 0)
        four = held([P, 1], F32, "four")
        nc.vector.memset(four[:], 4.0)

        kidx_sb = load_list(kidx, "kidx_sb")
        nc.sync.dma_start(d_bytes[:].bitcast(I32)[0:P:8, :], d_scales[0].bitcast(I32))
        offs_sb = load_list(offs, "offs_sb")
        x_rows = x_scales[0].bitcast(I32)
        for q in range(4):
            nc.sync.dma_start(x_bytes[:].bitcast(I32)[32 * q : 32 * q + 4, :], x_rows[4 * q : 4 * q + 4, :])
        half = held([P, 1], F32, "half")
        nc.scalar.activation(half[:], four[:], ACT.Abs_reciprocal_sqrt)
        d_table = held([P, G], U32, "d_table")
        nc.sync.dma_start(d_table[:].bitcast(I32), d_words[0].rearrange("p n r -> p (n r)").bitcast(I32))
        x_table = overlay.tile([P, T], U32, name="x_table", offset=2048, align_bytes=64)
        nc.sync.dma_start(x_table[:].bitcast(I32), x_words[0].rearrange("p n r -> p (n r)").bitcast(I32))
        w_table = held([P, 2 * N], U8, "w_table")
        nc.sync.dma_start(w_table[:].bitcast(I32), w1_words[0].bitcast(I32))
        w_rows = w1_scales[0].bitcast(I32)
        for q in range(4):
            nc.gpsimd.dma_start(w_bytes[:].bitcast(I32)[32 * q : 32 * q + 4, :], w_rows[4 * q : 4 * q + 4, :])
        n1_sb = load_list(n1, "n1_sb")
        n2_sb = load_list(n2, "n2_sb")
        n3_sb = load_list(n3, "n3_sb")
        gain = held([P, PACK], F32, "gain")
        nc.gpsimd.dma_start(gain[:], gn.rearrange("(p t) o -> p (t o)", t=PACK))
        n5_sb = load_list(n5, "n5_sb")
        n4_sb = load_list(n4, "n4_sb")

        key_bytes = held([P, H], U8, "key_bytes")
        nc.vector.tensor_copy(key_bytes[:], d_bytes[:].indirect(kidx_sb[:]))
        key_scale = held([P, H], U8, "key_scale")
        nc.vector.tensor_copy(
            key_scale[:].rearrange("p (t m) -> p t m", t=PACK),
            key_bytes[:].rearrange("p (m t) -> p t m", t=PACK),
        )
        for r in range(1, 4):
            nc.scalar.dma_start(key_scale[:].bitcast(I32)[r:P:32, :], key_scale[:].bitcast(I32)[8 * r : P : 32, :])
        query_scale = held([P, S], U8, "query_scale")
        nc.vector.tensor_copy(query_scale[:], x_bytes[:].indirect(offs_sb[:]))
        key_words = held([P, H], U32, "key_words")
        nc.vector.tensor_copy(key_words[:], d_table[:].indirect(kidx_sb[:]))
        keys_by_slot = key_words[:].bitcast(I32).rearrange("p (m t) -> p m t", t=PACK)
        key_first = held([P, P], U32, "key_first")
        nc.vector.tensor_copy(key_first[:].bitcast(I32), keys_by_slot[:, :, 0])
        query_words = held([P, S], U32, "query_words")
        for lo, hi in ((0, 256), (256, 512)):
            nc.vector.tensor_copy(query_words[:, lo:hi], x_table[:].indirect(entries(offs_sb, lo, hi)))

        key_rest = overlay.tile([P, 3 * P], U32, name="key_rest", offset=4096, align_bytes=64)
        nc.vector.tensor_copy(
            key_rest[:].bitcast(I32).rearrange("p (t m) -> p m t", t=PACK - 1), keys_by_slot[:, :, 1:PACK]
        )
        key_dealt = [key_first[:]] + [key_rest[:, t * P : (t + 1) * P] for t in range(PACK - 1)]
        w_dealt = overlay.tile([P, 2 * N], U8, name="w_dealt", offset=2048, align_bytes=64)
        nc.vector.tensor_copy(
            w_dealt[:].rearrange("p (t m b) -> p t m b", t=PACK, b=2),
            w_table[:].rearrange("p (m t b) -> p t m b", t=PACK, b=2),
        )
        w_scale = held([P, N], U8, "w_scale")
        nc.gpsimd.tensor_copy(
            w_scale[:].rearrange("p (t m) -> p t m", t=PACK),
            w_bytes[:].rearrange("p (m t) -> p t m", t=PACK),
        )
        factor = held([P, PACK], F32, "factor")
        nc.gpsimd.tensor_scalar(factor[:], gain[:], -0.0625, 0.0, ALU.mult, ALU.add)

        def score_matmul(bank, t, lo, hi):
            acc = psum.tile([P, hi - lo], F32, tag=f"bank{bank}", name=f"score{t}_{lo}")
            nc.tensor.matmul_mx(
                out=acc[:],
                lhsT=key_dealt[t].bitcast(FP8X4),
                lhsT_scale=key_scale[:, t * P : (t + 1) * P],
                rhs=query_words[:, lo:hi].bitcast(FP8X4),
                rhs_scale=query_scale[:, lo:hi],
                start=True,
                stop=True,
            )
            return acc

        score = [held([P, 2 * S if t < 2 else S], F32, f"score_window{t}") for t in range(PACK)]
        h_window = [held([P, S if t < 2 else 2 * S], F32, f"h_window{t}") for t in range(PACK)]
        size_window = [held([P, S if t < 2 else 2 * S], F32, f"size_window{t}") for t in range(PACK)]
        score_plain = [w[:, S : 2 * S] for w in (score[1], size_window[2], size_window[3], h_window[2])]
        for w in (score[0], h_window[3]):
            nc.scalar.copy(w[:, S : 2 * S], half[:].to_broadcast([P, S]))
        first = score_matmul(0, 0, 0, 256)
        second = score_matmul(1, 0, 256, 512)
        rest = [score_matmul(1 + t, t, 0, S) for t in range(1, PACK)]
        nc.scalar.copy(score[0][:, 0:256], first[:])
        nc.scalar.copy(score_plain[0][:, 0:256], first[:])
        nc.scalar.copy(score[0][:, 256:512], second[:])
        nc.scalar.copy(score_plain[0][:, 256:512], second[:])
        for t in range(1, PACK):
            nc.scalar.copy(score[t][:, 0:S], rest[t - 1][:])
            nc.scalar.copy(score_plain[t], rest[t - 1][:])

        size_plain = [held([P, S], F32, f"size_plain{t}") for t in range(PACK)]
        z_words = held([P, S], U32, "z_words")
        z_scale = held([P, S], U8, "z_scale")
        z_first = overlay.tile([P, 256, PACK], BF16, name="z_first", offset=0, align_bytes=64)
        z_second = held([P, 256, PACK], BF16, "z_second")

        units = [(0, 0, 512), (1, 0, 512), (2, 0, 256), (3, 0, 256), (2, 256, 512), (3, 256, 384), (3, 384, 512)]
        sums = {}
        gaps = {}

        def gather_sum(u):
            t, lo, hi = units[u]
            if u == 6:
                sums[u] = h_window[3][:, 0:128]
            else:
                sums[u] = ring.tile([P, hi - lo], F32, tag="sum", name=f"sum{u}")[:]
            nc.vector.tensor_tensor(
                sums[u], score[t][:].indirect(entries(n1_sb, lo, hi)), score_plain[t][:, lo:hi], ALU.add
            )

        def gather_gaps(u):
            t, lo, hi = units[u]
            gaps[u] = []
            for i, lst in enumerate((n2_sb, n3_sb)):
                if u == 5:
                    gap = overlay.tile([P, hi - lo], F32, name=f"gap{i}_{u}", offset=1024 * i, align_bytes=64)[:]
                elif u == 6:
                    gap = h_window[i][:, 0:128]
                else:
                    gap = ring.tile([P, hi - lo], F32, tag=f"gap{i}", name=f"gap{i}_{u}")[:]
                nc.vector.tensor_tensor(gap, score[t][:].indirect(entries(lst, lo, hi)), sums[u], ALU.subtract)
                gaps[u].append(gap)

        def larger_gap(u):
            t, lo, hi = units[u]
            if u == 6:
                larger = h_window[2][:, 0:128]
            else:
                larger = ring.tile([P, hi - lo], F32, tag="larger", name=f"larger{u}")[:]
            nc.vector.tensor_tensor(larger, gaps[u][0], gaps[u][1], ALU.max)
            if lo < 256:
                nc.scalar.activation(z_first[:, :, t], larger[:, 0:256], ACT.Copy, scale=factor[:, t : t + 1])
            if hi > 256:
                start = max(lo, 256)
                nc.scalar.activation(
                    z_second[:, start - 256 : hi - 256, t], larger[:, start - lo : hi - lo], ACT.Copy,
                    scale=factor[:, t : t + 1],
                )

        def second_product(source, lo, hi, parts):
            nc.vector.quantize_mx(
                out=z_words[:, lo:hi].bitcast(FP8X4),
                scales=z_scale[:, lo:hi],
                in_=source.rearrange("p n t -> p (n t)"),
            )
            for t in range(PACK):
                nc.tensor.matmul_mx(
                    out=parts[t],
                    lhsT=w_dealt[:, 2 * t * P : 2 * (t + 1) * P].bitcast(FP4X4),
                    lhsT_scale=w_scale[:, t * P : (t + 1) * P],
                    rhs=z_words[:, lo:hi].bitcast(FP8X4),
                    rhs_scale=z_scale[:, lo:hi],
                    start=True,
                    stop=True,
                )

        def first_sizes(t):
            nc.scalar.activation(size_window[t][:, 0:256], h_first[t], ACT.Abs)
            nc.sync.dma_start(size_plain[t][:, 0:256], size_window[t][:, 0:256])

        gather_sum(0)
        for u in range(len(units)):
            if u == 5:
                pair = [psum.tile([P, 2, 256], F32, tag=f"bank{5 + i}", name=f"h_first{i}") for i in range(2)]
                h_first = [pair[t // 2][:, t % 2, :] for t in range(PACK)]
                second_product(z_first[:], 0, 256, h_first)
            if u + 1 < len(units):
                gather_sum(u + 1)
            if u >= 1:
                larger_gap(u - 1)
            if u == 5:
                first_sizes(0)
                first_sizes(1)
            gather_gaps(u)
        nc.vector.tensor_copy(h_window[3][:, 0:256], h_first[3])
        larger_gap(len(units) - 1)
        first_sizes(2)
        first_sizes(3)

        lone = psum.tile([P, 128], F32, tag="bank7", name="h_lone")
        last = psum.tile([P, 128], F32, tag="bank0", name="h_last")
        both = [psum.tile([P, 256], F32, tag=f"bank{t}", name=f"h_both{t}") for t in range(1, PACK)]
        second_product(z_second[:, 0:128, :], 256, 384, [lone[:]] + [b[:, 0:128] for b in both])
        nc.scalar.activation(size_window[0][:, 256:384], lone[:], ACT.Abs)
        for t in range(2):
            nc.vector.tensor_copy(h_window[t][:, 0:256], h_first[t])
        second_product(z_second[:, 128:256, :], 384, 512, [last[:]] + [b[:, 128:256] for b in both])
        nc.scalar.activation(size_window[0][:, 384:512], last[:], ACT.Abs)
        nc.vector.tensor_copy(h_window[2][:, 0:256], h_first[2])
        for t in range(1, PACK):
            nc.scalar.activation(size_window[t][:, 256:512], both[t - 1][:], ACT.Abs)
        for t in range(2):
            nc.sync.dma_start(size_plain[t][:, 256:512], size_window[t][:, 256:512])

        def late_copies(t):
            if t == 0:
                nc.scalar.copy(h_window[0][:, 256:384], lone[:])
                nc.scalar.copy(h_window[0][:, 384:512], last[:])
            else:
                nc.scalar.copy(h_window[t][:, 256:512], both[t - 1][:])

        def late_sizes(t):
            nc.scalar.activation(size_plain[t][:, 256:512], both[t - 1][:], ACT.Abs)

        out_rows = out_0.rearrange("(p t) n -> p t n", t=PACK)
        out_words_dram = out_1[0].rearrange("p n r -> p (n r)").bitcast(I32)
        out_words = held([P, S], U32, "out_words")
        out_scale = held([P, S], U8, "out_scale")
        result = held([P, PACK, S], F32, "result")
        grouped = [held([P, 256, PACK], BF16, f"grouped{c}") for c in range(2)]
        out_units = [(0, 0, 256), (1, 0, 256), (2, 0, 512), (3, 0, 512), (0, 256, 512), (1, 256, 512)]
        inverse = {}

        def denominator(u):
            t, lo, hi = out_units[u]
            den = ring.tile([P, hi - lo], F32, tag="den", name=f"den{u}")
            nc.vector.tensor_tensor(
                den[:], size_window[t][:].indirect(entries(n5_sb, lo, hi)), size_plain[t][:, lo:hi], ALU.add
            )
            root = ring.tile([P, hi - lo], F32, tag="root", name=f"root{u}")
            nc.scalar.activation(root[:], den[:], ACT.Abs_reciprocal_sqrt, bias=half[:])
            inverse[u] = ring.tile([P, hi - lo], F32, tag="inverse", name=f"inverse{u}", bufs=6)
            nc.scalar.activation(inverse[u][:], root[:], ACT.Square)

        def quotient(u):
            t, lo, hi = out_units[u]
            nc.vector.tensor_tensor(
                result[:, t, lo:hi], h_window[t][:].indirect(entries(n4_sb, lo, hi)), inverse[u][:], ALU.mult
            )
            nc.sync.dma_start(out_rows[:, t, lo:hi], result[:, t, lo:hi])

        def quantise_out(c):
            lo, hi = 256 * c, 256 * (c + 1)
            nc.vector.quantize_mx(
                out=out_words[:, lo:hi].bitcast(FP8X4),
                scales=out_scale[:, lo:hi],
                in_=grouped[c][:].rearrange("p n t -> p (n t)"),
            )
            nc.sync.dma_start(out_words_dram[:, lo:hi], out_words[:, lo:hi].bitcast(I32))

        woven = result[:].rearrange("p t n -> p n t")
        late_sizes(2)
        denominator(0)
        late_copies(0)
        denominator(1)
        late_sizes(3)
        late_copies(1)
        denominator(2)
        quotient(0)
        late_copies(2)
        denominator(3)
        late_copies(3)
        quotient(1)
        quotient(2)
        denominator(4)
        quotient(3)
        nc.scalar.copy(grouped[0][:], woven[:, 0:256, :])
        denominator(5)
        quotient(4)
        quotient(5)
        quantise_out(0)
        nc.vector.tensor_copy(grouped[1][:, 0:160, :], woven[:, 256:416, :])
        nc.scalar.copy(grouped[1][:, 160:256, :], woven[:, 416:512, :])
        quantise_out(1)
        scale_rows = out_2[0].bitcast(I32)
        for q in range(4):
            queue = nc.scalar if q % 2 else nc.sync
            queue.dma_start(scale_rows[4 * q : 4 * q + 4, :], out_scale[:].bitcast(I32)[32 * q : 32 * q + 4, :])
